import numpy as np
import ml_dtypes


def mxq(x, axis, fmt="e4m3"):
    dtype, down = {"e4m3": (ml_dtypes.float8_e4m3fn, 7), "e5m2": (ml_dtypes.float8_e5m2, 14)}[fmt]
    v = np.moveaxis(np.asarray(x, np.float32).astype(ml_dtypes.bfloat16).astype(np.float64), axis, -1)
    blocks = v.reshape(v.shape[:-1] + (-1, 32))
    amax = np.abs(blocks).max(-1, keepdims=True)
    byte = np.maximum(np.where(amax > 0, np.frexp(amax)[1] - 1 + 127, 0) - down, 1)
    scale = np.exp2(byte - 127.0)
    codes = (blocks / scale).astype(np.float32).astype(dtype).astype(np.float64)
    return np.moveaxis((codes * scale).reshape(v.shape), -1, axis)


WIDE = False


def mx_kscale(k):
    if not WIDE:
        return np.ones(k)
    levels = np.array([10, -10, 5, -5, 0])
    if k % 512:
        return np.exp2(np.random.permutation(np.resize(levels, k // 32))).repeat(32)
    a = np.empty((k // 512, 16))
    for p in range(k // 512):
        a[p, :8] = np.random.permutation(np.resize(levels, 8))
        for g in range(8):
            far = levels[np.abs(levels - a[p, g]) >= 10]
            a[p, g + 8] = far[np.random.randint(len(far))]
    return np.exp2(a.ravel()).repeat(32)


def f64(x):
    return np.asarray(x).astype(np.float64)


def striped8(idx):
    return np.asarray(idx).reshape(8, -1, 16).transpose(0, 2, 1).reshape(128, -1).astype(np.uint16)


def unstriped8(offs):
    return offs.reshape(8, 16, -1).transpose(0, 2, 1).reshape(8, -1).astype(np.int64)


def pick8(x, idx, run):
    r = np.arange(len(x))
    return x[r[:, None], idx[r % (8 * run) // run]]


E2M1 = np.array([0.0, 0.5, 1.0, 1.5, 2.0, 3.0, 4.0, 6.0, -0.0, -0.5, -1.0, -1.5, -2.0, -3.0, -4.0, -6.0])


def pack_weight(w, fmt):
    k, n = w.shape
    w = f64(np.asarray(w, np.float32).astype(ml_dtypes.bfloat16)).reshape(k // 32, 32, n)
    amax = np.abs(w).max(1)
    if fmt == "e4m3":
        byte = np.frexp(amax)[1] - 1 + 127 - 7
    else:
        mant, ex = np.frexp(amax / 6.0)
        byte = np.where(mant > 0.5, ex, ex - 1) + 127
    byte = np.clip(np.where(amax > 0, byte, 1), 1, 254)
    scaled = (w * np.exp2(127.0 - byte)[:, None, :]).reshape(k, n).astype(np.float32)
    by_word = np.ascontiguousarray(scaled.reshape(k // 512, 128, 4, n).transpose(0, 1, 3, 2))
    if fmt == "e4m3":
        words = by_word.astype(ml_dtypes.float8_e4m3fn).view(np.uint8)
    else:
        c = by_word.astype(ml_dtypes.float4_e2m1fn).view(np.uint8) & 0xF
        words = (c[..., 0::2] | (c[..., 1::2] << 4)).reshape(k // 512, 128, 2 * n)
    return np.ascontiguousarray(words), np.ascontiguousarray(byte.astype(np.uint8).reshape(k // 512, 16, n))


def unpack_weight(words, scales, fmt):
    g, _, n = scales.shape
    words = np.ascontiguousarray(words).reshape(g, 128, n, -1)
    if fmt == "e4m3":
        vals = words.view(ml_dtypes.float8_e4m3fn).astype(np.float64)
    else:
        nib = np.empty((g, 128, n, 4), np.uint8)
        nib[..., 0::2] = words & 0xF
        nib[..., 1::2] = words >> 4
        vals = E2M1[nib]
    vals = vals * np.repeat(np.exp2(scales.astype(np.float64) - 127.0), 8, axis=1)[..., None]
    return vals.transpose(0, 1, 3, 2).reshape(g * 512, n)


D, T, I, Q = 512, 1024, 512, 128


def setup_inputs():
    n = np.random.standard_normal
    idx = np.stack([np.random.permutation(T)[:I] for _ in range(8)])
    idx2 = np.stack([np.random.permutation(T)[:I] for _ in range(8)])
    idx3 = np.stack([np.random.permutation(T)[:I] for _ in range(8)])
    fd = mx_kscale(D)
    keysp = pack_weight(n((D, T)) / fd[:, None], "e4m3")
    return {
        "query": (n((D, Q)) * 0.9 / np.sqrt(D) * fd[:, None]).astype(np.float32),
        "query2": (n((D, Q)) * 0.9 / np.sqrt(D) * fd[:, None]).astype(np.float32),
        "keys_words": keysp[0],
        "keys_scales": keysp[1],
        "lam": (np.random.uniform(0.5, 1.5, (Q, 1))).astype(np.float32),
        "old": (1.0 * n((Q, T))).astype(np.float32),
        "share2": (np.random.uniform(0.4, 1.2, (Q, 1))).astype(np.float32),
        "offs": striped8(idx),
        "offs2": striped8(idx2),
        "offs3": striped8(idx3),
    }


def reference(query, query2, keys_words, keys_scales, lam, old, share2, offs, offs2, offs3):
    idx = unstriped8(offs)
    idx2 = unstriped8(offs2)
    idx3 = unstriped8(offs3)
    keysu = unpack_weight(keys_words, keys_scales, "e4m3")
    queryq = mxq(f64(query), 0, "e4m3")
    a = queryq.T @ keysu
    query2q = mxq(f64(query2), 0, "e4m3")
    b = query2q.T @ keysu
    w = pick8(a, idx, 16) + pick8(a, idx2, 16) * np.tanh(pick8(b, idx, 16)) * f64(lam)
    f1 = np.zeros((Q, T))
    f1[np.arange(Q)[:, None], idx[np.arange(Q) % 128 // 16]] = w
    f2 = np.zeros((Q, T))
    f2[np.arange(Q)[:, None], idx3[np.arange(Q) % 128 // 16]] = w
    y = f64(old) + f1 + f2 * f64(share2)
    return y

@@ -1,0 +1,168 @@
+from contextlib import ExitStack
+
+import concourse.mybir as mybir
+from concourse.masks import make_identity
+
+D, T, SLOTS, Q = 512, 1024, 512, 128
+FLOPS = 2 * 2 * D * Q * T
+
+F32 = mybir.dt.float32
+BF16 = mybir.dt.bfloat16
+I32 = mybir.dt.int32
+U32 = mybir.dt.uint32
+U16 = mybir.dt.uint16
+U8 = mybir.dt.uint8
+FP8X4 = mybir.dt.float8_e4m3fn_x4
+ALU = mybir.AluOpType
+ACT = mybir.ActivationFunctionType
+
+P = 128
+PACK = 4
+BANK = 512
+HALF = SLOTS // 2
+LIST_COLS = SLOTS // 16
+
+
+def tile_attend_turnedby_lean_twiceput_heads_kernel(
+    tc, query, query2, keys_words, keys_scales, lam, old, share2, offs, offs2, offs3, out
+):
+    nc = tc.nc
+    with ExitStack() as ctx:
+        sb = ctx.enter_context(tc.tile_pool(name="sb", bufs=1))
+        ps = ctx.enter_context(tc.psum_pool(name="ps", bufs=1))
+
+        key_scales = sb.tile([P, T], U8, align_bytes=64)
+        nc.vector.memset(key_scales[:].bitcast(U32), 0)
+
+        words_hbm = keys_words[0].rearrange("p n r -> p (n r)")
+        key_words = [sb.tile([P, BANK], U32, align_bytes=64, name=f"key_words{h}") for h in range(2)]
+        q_raw = [sb.tile([P, PACK, Q], F32, name=f"q_raw{n}") for n in range(2)]
+        for n, q_hbm in enumerate((query2, query)):
+            nc.sync.dma_start(out=q_raw[n][:], in_=q_hbm.rearrange("(p j) w -> p j w", j=PACK))
+            if n == 0:
+                for quad in range(4):
+                    nc.sync.dma_start(
+                        out=key_scales[32 * quad : 32 * quad + 4, :].bitcast(I32),
+                        in_=keys_scales[0, 4 * quad : 4 * quad + 4, :].bitcast(I32),
+                    )
+            nc.sync.dma_start(
+                out=key_words[n][:].bitcast(I32),
+                in_=words_hbm[:, n * BANK * PACK : (n + 1) * BANK * PACK].bitcast(I32),
+            )
+        list1 = sb.tile([P, LIST_COLS], U16)
+        list2 = sb.tile([P, LIST_COLS], U16)
+        list3 = sb.tile([P, LIST_COLS], U16)
+        nc.sync.dma_start(list1[:], offs)
+        nc.sync.dma_start(list2[:], offs2)
+        nc.sync.dma_start(list3[:], offs3)
+        old_sb = sb.tile([P, T], F32)
+        nc.sync.dma_start(old_sb[:], old)
+
+        lam_sb = sb.tile([P, 1], F32)
+        share_sb = sb.tile([P, 1], F32)
+        nc.gpsimd.dma_start(lam_sb[:], lam)
+        nc.gpsimd.dma_start(share_sb[:], share2)
+        identity = sb.tile([P, P], F32)
+        make_identity(nc, identity[:])
+
+        put1 = sb.tile([P, T], F32)
+        put3 = sb.tile([P, T], F32)
+        nc.vector.memset(put1[:], 0.0)
+        nc.vector.memset(put3[:], 0.0)
+
+        q_codes, q_scales = [], []
+        for n in range(2):
+            grouped = sb.tile([P, Q, PACK], BF16, align_bytes=64, name=f"grouped{n}")
+            codes = sb.tile([P, Q], U32, align_bytes=64, name=f"q_codes{n}")
+            scales = sb.tile([P, Q], U8, align_bytes=64, name=f"q_scales{n}")
+            if n == 0:
+                nc.vector.tensor_copy(out=grouped[:], in_=q_raw[n][:].rearrange("p j w -> p w j"))
+            else:
+                nc.scalar.activation(grouped[:], q_raw[n][:].rearrange("p j w -> p w j"), ACT.Copy)
+            nc.vector.quantize_mx(
+                out=codes[:].bitcast(FP8X4), scales=scales[:], in_=grouped[:].rearrange("p w j -> p (w j)")
+            )
+            q_codes.append(codes)
+            q_scales.append(scales)
+
+        b_sb = sb.tile([P, T], F32)
+        a_sb = sb.tile([P, T], F32)
+
+        def score(n, dst, start, width, tag):
+            bank = ps.tile([P, BANK], F32, name=tag)
+            h, c = divmod(start, BANK)
+            nc.tensor.matmul_mx(
+                out=bank[:, :width],
+                lhsT=q_codes[n][:].bitcast(FP8X4),
+                lhsT_scale=q_scales[n][:],
+                rhs=key_words[h][:, c : c + width].bitcast(FP8X4),
+                rhs_scale=key_scales[:, start : start + width],
+                start=True,
+                stop=True,
+            )
+            nc.vector.tensor_copy(out=dst[:, start : start + width], in_=bank[:, :width])
+
+        score(0, b_sb, 0, BANK, "bank0")
+        score(0, b_sb, BANK, BANK, "bank1")
+        score(1, a_sb, 0, BANK, "bank2")
+        score(1, a_sb, BANK, BANK // 2, "bank3")
+        score(1, a_sb, BANK + BANK // 2, BANK // 2, "bank4")
+
+        picked_b = sb.tile([P, SLOTS], F32)
+        turn = sb.tile([P, SLOTS], F32)
+        direct = sb.tile([P, SLOTS], F32)
+        other = sb.tile([P, SLOTS], F32)
+        lean = sb.tile([P, SLOTS], F32)
+        slots = [slice(h * HALF, (h + 1) * HALF) for h in range(2)]
+        cols = [slice(h * LIST_COLS // 2, (h + 1) * LIST_COLS // 2) for h in range(2)]
+
+        for h in range(2):
+            nc.scalar.activation(picked_b[:, slots[h]], b_sb[:].indirect(list1[:, cols[h]]), ACT.Copy)
+            nc.scalar.activation(turn[:, slots[h]], picked_b[:, slots[h]], ACT.Tanh)
+            if h == 0:
+                nc.vector.tensor_copy(other[:, slots[h]], a_sb[:].indirect(list2[:, cols[h]]))
+            else:
+                nc.scalar.activation(other[:, slots[h]], a_sb[:].indirect(list2[:, cols[h]]), ACT.Copy)
+            nc.scalar.activation(direct[:, slots[h]], a_sb[:].indirect(list1[:, cols[h]]), ACT.Copy)
+            nc.vector.scalar_tensor_tensor(
+                lean[:, slots[h]], other[:, slots[h]], lam_sb[:], turn[:, slots[h]], ALU.mult, ALU.mult
+            )
+            nc.vector.tensor_tensor(
+                put1[:].indirect(list1[:, cols[h]]), direct[:, slots[h]], lean[:, slots[h]], ALU.add
+            )
+        direct_share = sb.tile([P, SLOTS], F32)
+        lean_share = sb.tile([P, SLOTS], F32)
+        nc.scalar.activation(direct_share[:], direct[:], ACT.Copy, scale=share_sb[:])
+        nc.scalar.activation(lean_share[:], lean[:], ACT.Copy, scale=share_sb[:])
+        nc.vector.tensor_tensor(put3[:].indirect(list3[:]), direct_share[:], lean_share[:], ALU.add)
+
+        blocks = BANK // P
+        turned = [ps.tile([P, BANK], F32, name=f"bank{3 + h}") for h in range(2)]
+        for src in (old_sb, put1):
+            for h in range(2):
+                for j in range(blocks):
+                    nc.tensor.matmul(
+                        turned[h][:, j * P : (j + 1) * P],
+                        src[:, h * BANK + j * P : h * BANK + (j + 1) * P],
+                        identity[:],
+                        start=(src is old_sb and j == 0),
+                        stop=(src is put1 and j == blocks - 1),
+                        is_transpose=True,
+                    )
+        turned_sb = sb.tile([P, T], F32)
+        result = sb.tile([P, T], F32)
+        for h in range(2):
+            nc.scalar.copy(turned_sb[:, h * BANK : (h + 1) * BANK], turned[h][:])
+            back = ps.tile([P, BANK], F32, name=f"bank{h}")
+            for j in range(blocks):
+                nc.tensor.transpose(
+                    back[:, j * P : (j + 1) * P],
+                    turned_sb[:, h * BANK + j * P : h * BANK + (j + 1) * P],
+                    identity[:],
+                )
+            for piece in range(2):
+                inside = slice(piece * BANK // 2, (piece + 1) * BANK // 2)
+                span = slice(h * BANK + inside.start, h * BANK + inside.stop)
+                nc.vector.tensor_tensor(result[:, span], back[:, inside], put3[:, span], ALU.add)
+                queue = nc.sync if piece == 0 else nc.scalar
+                queue.dma_start(out[:, span], result[:, span])

@@ -19,6 +19,7 @@ ACT = mybir.ActivationFunctionType
 P = 128
 PACK = 4
 BANK = 512
+PIECE = 256
 HALF = SLOTS // 2
 LIST_COLS = SLOTS // 16
 
@@ -35,19 +36,19 @@ def tile_attend_turnedby_lean_twiceput_heads_kernel(
         nc.vector.memset(key_scales[:].bitcast(U32), 0)
 
         words_hbm = keys_words[0].rearrange("p n r -> p (n r)")
-        key_words = [sb.tile([P, BANK], U32, align_bytes=64, name=f"key_words{h}") for h in range(2)]
+        key_words = [sb.tile([P, PIECE], U32, align_bytes=64, name=f"key_words{k}") for k in range(T // PIECE)]
         q_raw = [sb.tile([P, PACK, Q], F32, name=f"q_raw{n}") for n in range(2)]
-        for n, q_hbm in enumerate((query2, query)):
-            nc.sync.dma_start(out=q_raw[n][:], in_=q_hbm.rearrange("(p j) w -> p j w", j=PACK))
-            if n == 0:
-                for quad in range(4):
-                    nc.sync.dma_start(
-                        out=key_scales[32 * quad : 32 * quad + 4, :].bitcast(I32),
-                        in_=keys_scales[0, 4 * quad : 4 * quad + 4, :].bitcast(I32),
-                    )
+        nc.sync.dma_start(out=q_raw[0][:], in_=query2.rearrange("(p j) w -> p j w", j=PACK))
+        for quad in range(4):
             nc.sync.dma_start(
-                out=key_words[n][:].bitcast(I32),
-                in_=words_hbm[:, n * BANK * PACK : (n + 1) * BANK * PACK].bitcast(I32),
+                out=key_scales[32 * quad : 32 * quad + 4, :].bitcast(I32),
+                in_=keys_scales[0, 4 * quad : 4 * quad + 4, :].bitcast(I32),
+            )
+        nc.sync.dma_start(out=q_raw[1][:], in_=query.rearrange("(p j) w -> p j w", j=PACK))
+        for k in range(T // PIECE):
+            nc.sync.dma_start(
+                out=key_words[k][:].bitcast(I32),
+                in_=words_hbm[:, k * PIECE * PACK : (k + 1) * PIECE * PACK].bitcast(I32),
             )
         list1 = sb.tile([P, LIST_COLS], U16)
         list2 = sb.tile([P, LIST_COLS], U16)
@@ -56,14 +57,14 @@ def tile_attend_turnedby_lean_twiceput_heads_kernel(
         nc.sync.dma_start(list2[:], offs2)
         nc.sync.dma_start(list3[:], offs3)
         old_sb = sb.tile([P, T], F32)
-        nc.sync.dma_start(old_sb[:], old)
 
         lam_sb = sb.tile([P, 1], F32)
         share_sb = sb.tile([P, 1], F32)
-        nc.gpsimd.dma_start(lam_sb[:], lam)
-        nc.gpsimd.dma_start(share_sb[:], share2)
+        nc.sync.dma_start(share_sb[:], share2)
+        nc.sync.dma_start(old_sb[:], old)
         identity = sb.tile([P, P], F32)
         make_identity(nc, identity[:])
+        nc.gpsimd.dma_start(lam_sb[:], lam)
 
         put1 = sb.tile([P, T], F32)
         put3 = sb.tile([P, T], F32)
@@ -88,48 +89,45 @@ def tile_attend_turnedby_lean_twiceput_heads_kernel(
         b_sb = sb.tile([P, T], F32)
         a_sb = sb.tile([P, T], F32)
 
-        def score(n, dst, start, width, tag):
-            bank = ps.tile([P, BANK], F32, name=tag)
-            h, c = divmod(start, BANK)
-            nc.tensor.matmul_mx(
-                out=bank[:, :width],
-                lhsT=q_codes[n][:].bitcast(FP8X4),
-                lhsT_scale=q_scales[n][:],
-                rhs=key_words[h][:, c : c + width].bitcast(FP8X4),
-                rhs_scale=key_scales[:, start : start + width],
-                start=True,
-                stop=True,
-            )
-            nc.vector.tensor_copy(out=dst[:, start : start + width], in_=bank[:, :width])
-
-        score(0, b_sb, 0, BANK, "bank0")
-        score(0, b_sb, BANK, BANK, "bank1")
-        score(1, a_sb, 0, BANK, "bank2")
-        score(1, a_sb, BANK, BANK // 2, "bank3")
-        score(1, a_sb, BANK + BANK // 2, BANK // 2, "bank4")
+        for n, dst in enumerate((b_sb, a_sb)):
+            for k in range(T // PIECE):
+                span = slice(k * PIECE, (k + 1) * PIECE)
+                bank = ps.tile([P, BANK], F32, name=f"bank{n * (T // PIECE) + k}")
+                nc.tensor.matmul_mx(
+                    out=bank[:, :PIECE],
+                    lhsT=q_codes[n][:].bitcast(FP8X4),
+                    lhsT_scale=q_scales[n][:],
+                    rhs=key_words[k][:].bitcast(FP8X4),
+                    rhs_scale=key_scales[:, span],
+                    start=True,
+                    stop=True,
+                )
+                if n == 0 and k % 2 == 0:
+                    nc.scalar.copy(dst[:, span], bank[:, :PIECE])
+                else:
+                    nc.vector.tensor_copy(out=dst[:, span], in_=bank[:, :PIECE])
 
         picked_b = sb.tile([P, SLOTS], F32)
         turn = sb.tile([P, SLOTS], F32)
         direct = sb.tile([P, SLOTS], F32)
         other = sb.tile([P, SLOTS], F32)
         lean = sb.tile([P, SLOTS], F32)
-        slots = [slice(h * HALF, (h + 1) * HALF) for h in range(2)]
-        cols = [slice(h * LIST_COLS // 2, (h + 1) * LIST_COLS // 2) for h in range(2)]
-
         for h in range(2):
-            nc.scalar.activation(picked_b[:, slots[h]], b_sb[:].indirect(list1[:, cols[h]]), ACT.Copy)
-            nc.scalar.activation(turn[:, slots[h]], picked_b[:, slots[h]], ACT.Tanh)
+            slots = slice(h * HALF, (h + 1) * HALF)
+            cols = slice(h * LIST_COLS // 2, (h + 1) * LIST_COLS // 2)
+            nc.scalar.activation(picked_b[:, slots], b_sb[:].indirect(list1[:, cols]), ACT.Copy)
+            nc.scalar.activation(turn[:, slots], picked_b[:, slots], ACT.Tanh)
             if h == 0:
-                nc.vector.tensor_copy(other[:, slots[h]], a_sb[:].indirect(list2[:, cols[h]]))
+                nc.vector.tensor_copy(other[:, slots], a_sb[:].indirect(list2[:, cols]))
+                nc.vector.tensor_copy(direct[:, slots], a_sb[:].indirect(list1[:, cols]))
             else:
-                nc.scalar.activation(other[:, slots[h]], a_sb[:].indirect(list2[:, cols[h]]), ACT.Copy)
-            nc.scalar.activation(direct[:, slots[h]], a_sb[:].indirect(list1[:, cols[h]]), ACT.Copy)
+                nc.scalar.activation(other[:, slots], a_sb[:].indirect(list2[:, cols]), ACT.Copy)
+                nc.scalar.activation(direct[:, slots], a_sb[:].indirect(list1[:, cols]), ACT.Copy)
             nc.vector.scalar_tensor_tensor(
-                lean[:, slots[h]], other[:, slots[h]], lam_sb[:], turn[:, slots[h]], ALU.mult, ALU.mult
+                lean[:, slots], other[:, slots], lam_sb[:], turn[:, slots], ALU.mult, ALU.mult
             )
-            nc.vector.tensor_tensor(
-                put1[:].indirect(list1[:, cols[h]]), direct[:, slots[h]], lean[:, slots[h]], ALU.add
-            )
+            nc.vector.tensor_tensor(put1[:].indirect(list1[:, cols]), direct[:, slots], lean[:, slots], ALU.add)
+
         direct_share = sb.tile([P, SLOTS], F32)
         lean_share = sb.tile([P, SLOTS], F32)
         nc.scalar.activation(direct_share[:], direct[:], ACT.Copy, scale=share_sb[:])
@@ -137,7 +135,7 @@ def tile_attend_turnedby_lean_twiceput_heads_kernel(
         nc.vector.tensor_tensor(put3[:].indirect(list3[:]), direct_share[:], lean_share[:], ALU.add)
 
         blocks = BANK // P
-        turned = [ps.tile([P, BANK], F32, name=f"bank{3 + h}") for h in range(2)]
+        turned = [ps.tile([P, BANK], F32, name=f"bank{6 + h}") for h in range(2)]
         for src in (old_sb, put1):
             for h in range(2):
                 for j in range(blocks):

@@ -102,7 +102,7 @@ def tile_attend_turnedby_lean_twiceput_heads_kernel(
                     start=True,
                     stop=True,
                 )
-                if n == 0 and k % 2 == 0:
+                if n == 0 and k < 3:
                     nc.scalar.copy(dst[:, span], bank[:, :PIECE])
                 else:
                     nc.vector.tensor_copy(out=dst[:, span], in_=bank[:, :PIECE])
@@ -110,7 +110,7 @@ def tile_attend_turnedby_lean_twiceput_heads_kernel(
         picked_b = sb.tile([P, SLOTS], F32)
         turn = sb.tile([P, SLOTS], F32)
         direct = sb.tile([P, SLOTS], F32)
-        other = sb.tile([P, SLOTS], F32)
+        other = sb.tile([P, HALF], F32)
         lean = sb.tile([P, SLOTS], F32)
         for h in range(2):
             slots = slice(h * HALF, (h + 1) * HALF)
@@ -118,13 +118,13 @@ def tile_attend_turnedby_lean_twiceput_heads_kernel(
             nc.scalar.activation(picked_b[:, slots], b_sb[:].indirect(list1[:, cols]), ACT.Copy)
             nc.scalar.activation(turn[:, slots], picked_b[:, slots], ACT.Tanh)
             if h == 0:
-                nc.vector.tensor_copy(other[:, slots], a_sb[:].indirect(list2[:, cols]))
+                nc.vector.tensor_copy(other[:], a_sb[:].indirect(list2[:, cols]))
                 nc.vector.tensor_copy(direct[:, slots], a_sb[:].indirect(list1[:, cols]))
             else:
-                nc.scalar.activation(other[:, slots], a_sb[:].indirect(list2[:, cols]), ACT.Copy)
                 nc.scalar.activation(direct[:, slots], a_sb[:].indirect(list1[:, cols]), ACT.Copy)
+                nc.scalar.activation(other[:], a_sb[:].indirect(list2[:, cols]), ACT.Copy)
             nc.vector.scalar_tensor_tensor(
-                lean[:, slots], other[:, slots], lam_sb[:], turn[:, slots], ALU.mult, ALU.mult
+                lean[:, slots], other[:], lam_sb[:], turn[:, slots], ALU.mult, ALU.mult
             )
             nc.vector.tensor_tensor(put1[:].indirect(list1[:, cols]), direct[:, slots], lean[:, slots], ALU.add)
 
@@ -134,33 +134,37 @@ def tile_attend_turnedby_lean_twiceput_heads_kernel(
         nc.scalar.activation(lean_share[:], lean[:], ACT.Copy, scale=share_sb[:])
         nc.vector.tensor_tensor(put3[:].indirect(list3[:]), direct_share[:], lean_share[:], ALU.add)
 
-        blocks = BANK // P
-        turned = [ps.tile([P, BANK], F32, name=f"bank{6 + h}") for h in range(2)]
+        pieces = T // PIECE
+        blocks = PIECE // P
+        turned = [ps.tile([P, BANK], F32, name=f"bank{pieces + k}") for k in range(pieces)]
         for src in (old_sb, put1):
-            for h in range(2):
+            for k in range(pieces):
                 for j in range(blocks):
                     nc.tensor.matmul(
-                        turned[h][:, j * P : (j + 1) * P],
-                        src[:, h * BANK + j * P : h * BANK + (j + 1) * P],
+                        turned[k][:, j * P : (j + 1) * P],
+                        src[:, k * PIECE + j * P : k * PIECE + (j + 1) * P],
                         identity[:],
                         start=(src is old_sb and j == 0),
                         stop=(src is put1 and j == blocks - 1),
                         is_transpose=True,
                     )
         turned_sb = sb.tile([P, T], F32)
+        first_sum = sb.tile([P, PIECE], F32)
         result = sb.tile([P, T], F32)
-        for h in range(2):
-            nc.scalar.copy(turned_sb[:, h * BANK : (h + 1) * BANK], turned[h][:])
-            back = ps.tile([P, BANK], F32, name=f"bank{h}")
+        for k in range(pieces):
+            span = slice(k * PIECE, (k + 1) * PIECE)
+            nc.scalar.copy(turned_sb[:, span], turned[k][:, :PIECE])
+            back = ps.tile([P, BANK], F32, name=f"bank{k}")
             for j in range(blocks):
                 nc.tensor.transpose(
                     back[:, j * P : (j + 1) * P],
-                    turned_sb[:, h * BANK + j * P : h * BANK + (j + 1) * P],
+                    turned_sb[:, k * PIECE + j * P : k * PIECE + (j + 1) * P],
                     identity[:],
                 )
-            for piece in range(2):
-                inside = slice(piece * BANK // 2, (piece + 1) * BANK // 2)
-                span = slice(h * BANK + inside.start, h * BANK + inside.stop)
-                nc.vector.tensor_tensor(result[:, span], back[:, inside], put3[:, span], ALU.add)
-                queue = nc.sync if piece == 0 else nc.scalar
-                queue.dma_start(out[:, span], result[:, span])
+            if k == 0:
+                nc.scalar.copy(first_sum[:], back[:, :PIECE])
+                nc.gpsimd.tensor_tensor(result[:, span], first_sum[:], put3[:, span], ALU.add)
+            else:
+                nc.vector.tensor_tensor(result[:, span], back[:, :PIECE], put3[:, span], ALU.add)
+            queue = nc.scalar if k == 0 else nc.sync
+            queue.dma_start(out[:, span], result[:, span])

from contextlib import ExitStack

import concourse.mybir as mybir
from concourse.masks import make_identity

D, T, SLOTS, Q = 512, 1024, 512, 128
FLOPS = 2 * 2 * D * Q * T

F32 = mybir.dt.float32
BF16 = mybir.dt.bfloat16
I32 = mybir.dt.int32
U32 = mybir.dt.uint32
U16 = mybir.dt.uint16
U8 = mybir.dt.uint8
FP8X4 = mybir.dt.float8_e4m3fn_x4
ALU = mybir.AluOpType
ACT = mybir.ActivationFunctionType

P = 128
PACK = 4
BANK = 512
PIECE = 256
HALF = SLOTS // 2
LIST_COLS = SLOTS // 16


def tile_attend_turnedby_lean_twiceput_heads_kernel(
    tc, query, query2, keys_words, keys_scales, lam, old, share2, offs, offs2, offs3, out
):
    nc = tc.nc
    with ExitStack() as ctx:
        sb = ctx.enter_context(tc.tile_pool(name="sb", bufs=1))
        ps = ctx.enter_context(tc.psum_pool(name="ps", bufs=1))

        key_scales = sb.tile([P, T], U8, align_bytes=64)
        nc.vector.memset(key_scales[:].bitcast(U32), 0)

        words_hbm = keys_words[0].rearrange("p n r -> p (n r)")
        key_words = [sb.tile([P, PIECE], U32, align_bytes=64, name=f"key_words{k}") for k in range(T // PIECE)]
        q_raw = [sb.tile([P, PACK, Q], F32, name=f"q_raw{n}") for n in range(2)]
        nc.sync.dma_start(out=q_raw[0][:], in_=query2.rearrange("(p j) w -> p j w", j=PACK))
        for quad in range(4):
            nc.sync.dma_start(
                out=key_scales[32 * quad : 32 * quad + 4, :].bitcast(I32),
                in_=keys_scales[0, 4 * quad : 4 * quad + 4, :].bitcast(I32),
            )
        nc.sync.dma_start(out=q_raw[1][:], in_=query.rearrange("(p j) w -> p j w", j=PACK))
        for k in range(T // PIECE):
            nc.sync.dma_start(
                out=key_words[k][:].bitcast(I32),
                in_=words_hbm[:, k * PIECE * PACK : (k + 1) * PIECE * PACK].bitcast(I32),
            )
        list1 = sb.tile([P, LIST_COLS], U16)
        list2 = sb.tile([P, LIST_COLS], U16)
        list3 = sb.tile([P, LIST_COLS], U16)
        nc.sync.dma_start(list1[:], offs)
        nc.sync.dma_start(list2[:], offs2)
        nc.sync.dma_start(list3[:], offs3)
        old_sb = sb.tile([P, T], F32)

        lam_sb = sb.tile([P, 1], F32)
        share_sb = sb.tile([P, 1], F32)
        nc.sync.dma_start(share_sb[:], share2)
        nc.sync.dma_start(old_sb[:], old)
        identity = sb.tile([P, P], F32)
        make_identity(nc, identity[:])
        nc.gpsimd.dma_start(lam_sb[:], lam)

        put1 = sb.tile([P, T], F32)
        put3 = sb.tile([P, T], F32)
        nc.vector.memset(put1[:], 0.0)
        nc.vector.memset(put3[:], 0.0)

        q_codes, q_scales = [], []
        for n in range(2):
            grouped = sb.tile([P, Q, PACK], BF16, align_bytes=64, name=f"grouped{n}")
            codes = sb.tile([P, Q], U32, align_bytes=64, name=f"q_codes{n}")
            scales = sb.tile([P, Q], U8, align_bytes=64, name=f"q_scales{n}")
            if n == 0:
                nc.vector.tensor_copy(out=grouped[:], in_=q_raw[n][:].rearrange("p j w -> p w j"))
            else:
                nc.scalar.activation(grouped[:], q_raw[n][:].rearrange("p j w -> p w j"), ACT.Copy)
            nc.vector.quantize_mx(
                out=codes[:].bitcast(FP8X4), scales=scales[:], in_=grouped[:].rearrange("p w j -> p (w j)")
            )
            q_codes.append(codes)
            q_scales.append(scales)

        b_sb = sb.tile([P, T], F32)
        a_sb = sb.tile([P, T], F32)

        for n, dst in enumerate((b_sb, a_sb)):
            for k in range(T // PIECE):
                span = slice(k * PIECE, (k + 1) * PIECE)
                bank = ps.tile([P, BANK], F32, name=f"bank{n * (T // PIECE) + k}")
                nc.tensor.matmul_mx(
                    out=bank[:, :PIECE],
                    lhsT=q_codes[n][:].bitcast(FP8X4),
                    lhsT_scale=q_scales[n][:],
                    rhs=key_words[k][:].bitcast(FP8X4),
                    rhs_scale=key_scales[:, span],
                    start=True,
                    stop=True,
                )
                if n == 0 and k < 3:
                    nc.scalar.copy(dst[:, span], bank[:, :PIECE])
                else:
                    nc.vector.tensor_copy(out=dst[:, span], in_=bank[:, :PIECE])

        picked_b = sb.tile([P, SLOTS], F32)
        turn = sb.tile([P, SLOTS], F32)
        direct = sb.tile([P, SLOTS], F32)
        other = sb.tile([P, HALF], F32)
        lean = sb.tile([P, SLOTS], F32)
        for h in range(2):
            slots = slice(h * HALF, (h + 1) * HALF)
            cols = slice(h * LIST_COLS // 2, (h + 1) * LIST_COLS // 2)
            nc.scalar.activation(picked_b[:, slots], b_sb[:].indirect(list1[:, cols]), ACT.Copy)
            nc.scalar.activation(turn[:, slots], picked_b[:, slots], ACT.Tanh)
            if h == 0:
                nc.vector.tensor_copy(other[:], a_sb[:].indirect(list2[:, cols]))
                nc.vector.tensor_copy(direct[:, slots], a_sb[:].indirect(list1[:, cols]))
            else:
                nc.scalar.activation(direct[:, slots], a_sb[:].indirect(list1[:, cols]), ACT.Copy)
                nc.scalar.activation(other[:], a_sb[:].indirect(list2[:, cols]), ACT.Copy)
            nc.vector.scalar_tensor_tensor(
                lean[:, slots], other[:], lam_sb[:], turn[:, slots], ALU.mult, ALU.mult
            )
            nc.vector.tensor_tensor(put1[:].indirect(list1[:, cols]), direct[:, slots], lean[:, slots], ALU.add)

        direct_share = sb.tile([P, SLOTS], F32)
        lean_share = sb.tile([P, SLOTS], F32)
        nc.scalar.activation(direct_share[:], direct[:], ACT.Copy, scale=share_sb[:])
        nc.scalar.activation(lean_share[:], lean[:], ACT.Copy, scale=share_sb[:])
        nc.vector.tensor_tensor(put3[:].indirect(list3[:]), direct_share[:], lean_share[:], ALU.add)

        pieces = T // PIECE
        blocks = PIECE // P
        turned = [ps.tile([P, BANK], F32, name=f"bank{pieces + k}") for k in range(pieces)]
        for src in (old_sb, put1):
            for k in range(pieces):
                for j in range(blocks):
                    nc.tensor.matmul(
                        turned[k][:, j * P : (j + 1) * P],
                        src[:, k * PIECE + j * P : k * PIECE + (j + 1) * P],
                        identity[:],
                        start=(src is old_sb and j == 0),
                        stop=(src is put1 and j == blocks - 1),
                        is_transpose=True,
                    )
        turned_sb = sb.tile([P, T], F32)
        first_sum = sb.tile([P, PIECE], F32)
        result = sb.tile([P, T], F32)
        for k in range(pieces):
            span = slice(k * PIECE, (k + 1) * PIECE)
            nc.scalar.copy(turned_sb[:, span], turned[k][:, :PIECE])
            back = ps.tile([P, BANK], F32, name=f"bank{k}")
            for j in range(blocks):
                nc.tensor.transpose(
                    back[:, j * P : (j + 1) * P],
                    turned_sb[:, k * PIECE + j * P : k * PIECE + (j + 1) * P],
                    identity[:],
                )
            if k == 0:
                nc.scalar.copy(first_sum[:], back[:, :PIECE])
                nc.gpsimd.tensor_tensor(result[:, span], first_sum[:], put3[:, span], ALU.add)
            else:
                nc.vector.tensor_tensor(result[:, span], back[:, :PIECE], put3[:, span], ALU.add)
            queue = nc.scalar if k == 0 else nc.sync
            queue.dma_start(out[:, span], result[:, span])
